import numpy as np
import ml_dtypes


def mxq(x, axis, fmt="e4m3"):
    dtype, down = {"e4m3": (ml_dtypes.float8_e4m3fn, 7), "e5m2": (ml_dtypes.float8_e5m2, 14)}[fmt]
    v = np.moveaxis(np.asarray(x, np.float32).astype(ml_dtypes.bfloat16).astype(np.float64), axis, -1)
    blocks = v.reshape(v.shape[:-1] + (-1, 32))
    amax = np.abs(blocks).max(-1, keepdims=True)
    byte = np.maximum(np.where(amax > 0, np.frexp(amax)[1] - 1 + 127, 0) - down, 1)
    scale = np.exp2(byte - 127.0)
    codes = (blocks / scale).astype(np.float32).astype(dtype).astype(np.float64)
    return np.moveaxis((codes * scale).reshape(v.shape), -1, axis)


WIDE = False


def mx_kscale(k):
    if not WIDE:
        return np.ones(k)
    levels = np.array([30, -30])
    if k % 512:
        return np.exp2(np.random.permutation(np.resize(levels, k // 32))).repeat(32)
    a = np.empty((k // 512, 16))
    for p in range(k // 512):
        a[p, :8] = np.random.permutation(np.resize(levels, 8))
        for g in range(8):
            far = levels[np.abs(levels - a[p, g]) >= 10]
            a[p, g + 8] = far[np.random.randint(len(far))]
    return np.exp2(a.ravel()).repeat(32)


def f64(x):
    return np.asarray(x).astype(np.float64)


def striped(idx):
    return np.tile(np.asarray(idx).reshape(-1, 16).T, (8, 1)).astype(np.uint16)


def unstriped(offs):
    return offs[:16].T.reshape(-1).astype(np.int64)


E2M1 = np.array([0.0, 0.5, 1.0, 1.5, 2.0, 3.0, 4.0, 6.0, -0.0, -0.5, -1.0, -1.5, -2.0, -3.0, -4.0, -6.0])


def pack_weight(w, fmt):
    k, n = w.shape
    w = f64(np.asarray(w, np.float32).astype(ml_dtypes.bfloat16)).reshape(k // 32, 32, n)
    amax = np.abs(w).max(1)
    if fmt in ("e4m3", "e5m2"):
        byte = np.frexp(amax)[1] - 1 + 127 - (7 if fmt == "e4m3" else 14)
    else:
        mant, ex = np.frexp(amax / 6.0)
        byte = np.where(mant > 0.5, ex, ex - 1) + 127
    byte = np.clip(np.where(amax > 0, byte, 1), 1, 254)
    scaled = (w * np.exp2(127.0 - byte)[:, None, :]).reshape(k, n).astype(np.float32)
    by_word = np.ascontiguousarray(scaled.reshape(k // 512, 128, 4, n).transpose(0, 1, 3, 2))
    if fmt in ("e4m3", "e5m2"):
        words = by_word.astype(ml_dtypes.float8_e4m3fn if fmt == "e4m3" else ml_dtypes.float8_e5m2).view(np.uint8)
    else:
        c = by_word.astype(ml_dtypes.float4_e2m1fn).view(np.uint8) & 0xF
        words = (c[..., 0::2] | (c[..., 1::2] << 4)).reshape(k // 512, 128, 2 * n)
    return np.ascontiguousarray(words), np.ascontiguousarray(byte.astype(np.uint8).reshape(k // 512, 16, n))


def unpack_weight(words, scales, fmt):
    g, _, n = scales.shape
    words = np.ascontiguousarray(words).reshape(g, 128, n, -1)
    if fmt in ("e4m3", "e5m2"):
        vals = words.view(ml_dtypes.float8_e4m3fn if fmt == "e4m3" else ml_dtypes.float8_e5m2).astype(np.float64)
    else:
        nib = np.empty((g, 128, n, 4), np.uint8)
        nib[..., 0::2] = words & 0xF
        nib[..., 1::2] = words >> 4
        vals = E2M1[nib]
    vals = vals * np.repeat(np.exp2(scales.astype(np.float64) - 127.0), 8, axis=1)[..., None]
    return vals.transpose(0, 1, 3, 2).reshape(g * 512, n)


K, T, Z, J, R, C, O, N, E = 512, 1024, 1024, 256, 512, 512, 256, 256, 128


def setup_inputs():
    n = np.random.standard_normal
    idx = np.random.permutation(T)[:J]
    idx2 = np.random.permutation(Z)[:J]
    idx3 = np.random.permutation(C)[:J]
    idx4 = np.random.permutation(C)[:J]
    idx5 = np.random.permutation(C)[:O]
    idx6 = np.random.permutation(O)[:E]
    idx7 = np.random.permutation(O)[:E]
    fk = mx_kscale(K)
    fr = mx_kscale(R)
    xtp = pack_weight(n((K, T)) / fk[:, None], "e2m1")
    xop = pack_weight(n((K, Z)) / fk[:, None], "e4m3")
    wp = pack_weight(n((K, R)) * 1 / np.sqrt(K) * fk[:, None] * fr, "e4m3")
    w2p = pack_weight(n((K, R)) * 1 / np.sqrt(K) * fk[:, None] * fr, "e5m2")
    wbp = pack_weight(n((R, N)) * 1 / np.sqrt(R) / fr[:, None], "e2m1")
    return {
        "xt_words": xtp[0],
        "xt_scales": xtp[1],
        "xo_words": xop[0],
        "xo_scales": xop[1],
        "w_words": wp[0],
        "w_scales": wp[1],
        "w2_words": w2p[0],
        "w2_scales": w2p[1],
        "wb_words": wbp[0],
        "wb_scales": wbp[1],
        "offs": striped(idx),
        "offs2": striped(idx2),
        "offs3": striped(idx3),
        "offs4": striped(idx4),
        "offs5": striped(idx5),
        "offs6": striped(idx6),
        "offs7": striped(idx7),
    }


def reference(xt_words, xt_scales, xo_words, xo_scales, w_words, w_scales, w2_words, w2_scales, wb_words, wb_scales, offs, offs2, offs3, offs4, offs5, offs6, offs7):
    idx = unstriped(offs)
    idx2 = unstriped(offs2)
    idx3 = unstriped(offs3)
    idx4 = unstriped(offs4)
    idx5 = unstriped(offs5)
    idx6 = unstriped(offs6)
    idx7 = unstriped(offs7)
    xtu = unpack_weight(xt_words, xt_scales, "e2m1")
    xou = unpack_weight(xo_words, xo_scales, "e4m3")
    wu = unpack_weight(w_words, w_scales, "e4m3")
    w2u = unpack_weight(w2_words, w2_scales, "e5m2")
    wbu = unpack_weight(wb_words, wb_scales, "e2m1")
    xtidxg = xtu[:, idx]
    xoidx2g = xou[:, idx2]
    a = wu.T @ xtidxg + w2u.T @ xoidx2g
    b = w2u.T @ xtidxg + wu.T @ xoidx2g
    pw = np.zeros((R, C))
    pw[:, idx3] = a
    pv = np.zeros((R, C))
    pv[:, idx4] = b
    pg = pw + pv
    hid = pg[:, idx5]
    hidq = mxq(hid, 0, "e5m2")
    p = wbu.T @ hidq
    y = np.maximum(p[:, idx6], p[:, idx7])
    return y

@@ -1,0 +1,223 @@
+from contextlib import ExitStack
+
+import concourse.mybir as mybir
+
+K, T, Z, J, R, C, O, N, E = 512, 1024, 1024, 256, 512, 512, 256, 256, 128
+FLOPS = 2 * (4 * K * R * J + R * N * O)
+
+F32 = mybir.dt.float32
+BF16 = mybir.dt.bfloat16
+I32 = mybir.dt.int32
+U32 = mybir.dt.uint32
+U16 = mybir.dt.uint16
+U8 = mybir.dt.uint8
+E4M3 = mybir.dt.float8_e4m3fn_x4
+E5M2 = mybir.dt.float8_e5m2_x4
+E2M1 = mybir.dt.float4_e2m1fn_x4
+COPY = mybir.ActivationFunctionType.Copy
+ADD = mybir.AluOpType.add
+MAX = mybir.AluOpType.max
+
+P = 128
+PACK = 4
+PERIOD = 14
+
+
+def repeated(rows, times):
+    return rows.unsqueeze(0).to_broadcast([times, rows.shape[0], rows.shape[1]])
+
+
+def load_scales(queue, plane, scales):
+    rows = scales[0].bitcast(I32)
+    words = plane.bitcast(I32)
+    queue.dma_start(out=words[0 : PERIOD * 5, :], in_=repeated(rows[0:PERIOD, :], 5))
+    queue.dma_start(out=words[96:100, :], in_=rows[12:16, :])
+
+
+def load_scales_everywhere(queue, plane, scales):
+    rows = scales[0].bitcast(I32)
+    words = plane.bitcast(I32)
+    queue.dma_start(out=words[0 : PERIOD * 7, :], in_=repeated(rows[0:PERIOD, :], 7))
+    queue.dma_start(out=words[PERIOD * 7 : P, :], in_=repeated(rows[PERIOD:16, :], 15))
+
+
+def tile_list_crossed_shared_one_bestoftwo_kernel(
+    tc, xt_words, xt_scales, xo_words, xo_scales, w_words, w_scales, w2_words, w2_scales,
+    wb_words, wb_scales, offs, offs2, offs3, offs4, offs5, offs6, offs7, out,
+):
+    nc = tc.nc
+    with ExitStack() as ctx:
+        keep = ctx.enter_context(tc.tile_pool(name="keep", bufs=1))
+        psum = ctx.enter_context(tc.psum_pool(name="psum", bufs=1))
+
+        def tile(name, shape, dtype):
+            return keep.tile(shape, dtype, name=name, align_bytes=64)
+
+        def load_list(name, source):
+            held = keep.tile(list(source.shape), U16, name=name)
+            nc.sync.dma_start(held[:], source)
+            return held
+
+        def load_words(queue, name, source, shape, dtype):
+            held = tile(name, shape, dtype)
+            queue.dma_start(out=held[:].bitcast(I32), in_=source.bitcast(I32))
+            return held
+
+        xt_plane = tile("xt_plane", [P, T], U8)
+        xo_plane = tile("xo_plane", [P, Z], U8)
+        w_planes = tile("w_planes", [P, 2 * R], U8)
+        wb_plane = tile("wb_plane", [P, N], U8)
+        for plane in (xt_plane, xo_plane, wb_plane):
+            nc.vector.memset(plane[:].bitcast(I32), 0)
+        load_scales_everywhere(nc.gpsimd, w_planes[:, 0:R], w_scales)
+        load_scales_everywhere(nc.gpsimd, w_planes[:, R : 2 * R], w2_scales)
+        board_a = [tile("board_a%d" % t, [P, C], F32) for t in range(PACK)]
+        board_b = [tile("board_b%d" % t, [P, C], F32) for t in range(PACK)]
+        for t in range(PACK):
+            nc.gpsimd.memset(board_a[t][:], 0.0)
+            nc.gpsimd.memset(board_b[t][:], 0.0)
+
+        list1 = load_list("list1", offs)
+        w_codes = load_words(nc.scalar, "w_codes", w_words[0].rearrange("p n t -> p (n t)"), [P, R], U32)
+        w2_codes = load_words(nc.scalar, "w2_codes", w2_words[0].rearrange("p n t -> p (n t)"), [P, R], U32)
+        xt_codes = load_words(nc.scalar, "xt_codes", xt_words[0], [P, T], U16)
+        xo_codes = load_words(nc.scalar, "xo_codes", xo_words[0].rearrange("p n t -> p (n t)"), [P, Z], U32)
+        list2 = load_list("list2", offs2)
+        load_scales(nc.sync, xt_plane[:], xt_scales)
+        load_scales(nc.sync, xo_plane[:], xo_scales)
+        list3 = load_list("list3", offs3)
+        list4 = load_list("list4", offs4)
+        list5 = load_list("list5", offs5)
+        wb_codes = load_words(nc.sync, "wb_codes", wb_words[0], [P, 2 * N], U8)
+        load_scales(nc.sync, wb_plane[:], wb_scales)
+        list6 = load_list("list6", offs6)
+        list7 = load_list("list7", offs7)
+
+        w_dealt = tile("w_dealt", [P, R], U32)
+        w2_dealt = tile("w2_dealt", [P, R], U32)
+        for dealt, codes in ((w_dealt, w_codes), (w2_dealt, w2_codes)):
+            nc.scalar.copy(
+                dealt[:].rearrange("p (t c i) -> p c t i", t=PACK, i=4),
+                codes[:].rearrange("p (c i t) -> p c t i", t=PACK, i=4),
+            )
+
+        xt_pick = tile("xt_pick", [P, J], U16)
+        xt_pick_s = tile("xt_pick_s", [P, J], U8)
+        xo_pick = tile("xo_pick", [P, J], U32)
+        xo_pick_s = tile("xo_pick_s", [P, J], U8)
+        nc.vector.tensor_copy(xt_pick_s[:], xt_plane[:].indirect(list1[:]))
+        nc.vector.tensor_copy(xt_pick[:], xt_codes[:].indirect(list1[:]))
+        nc.vector.tensor_copy(xo_pick_s[:], xo_plane[:].indirect(list2[:]))
+        nc.vector.tensor_copy(xo_pick[:], xo_codes[:].indirect(list2[:]))
+
+        by_slot = w_planes[:].rearrange("p (c i t) -> p c t i", t=PACK, i=16)
+        planes_first = tile("planes_first", [P, 2 * P], U8)
+        planes_rest = tile("planes_rest", [P, (PACK - 1) * 2 * P], U8)
+        nc.vector.tensor_copy(planes_first[:].rearrange("p (c i) -> p c i", i=16), by_slot[:, :, 0, :])
+        nc.vector.tensor_copy(
+            planes_rest[:].rearrange("p (t c i) -> p c t i", t=PACK - 1, i=16), by_slot[:, :, 1:PACK, :]
+        )
+
+        def weight(which, t):
+            codes, fmt = ((w_dealt, E4M3), (w2_dealt, E5M2))[which]
+            if t == 0:
+                plane = planes_first[:, which * P : (which + 1) * P]
+            else:
+                start = (2 * (t - 1) + which) * P
+                plane = planes_rest[:, start : start + P]
+            return codes[:, t * P : (t + 1) * P].bitcast(fmt), plane
+
+        moving = ((xt_pick[:].bitcast(E2M1), xt_pick_s[:]), (xo_pick[:].bitcast(E4M3), xo_pick_s[:]))
+
+        def product(name, t, crossed):
+            acc = psum.tile([P, J], F32, name=name)
+            for side in range(2):
+                lhs, lhs_scale = weight(side ^ crossed, t)
+                rhs, rhs_scale = moving[side]
+                nc.tensor.matmul_mx(out=acc[:], lhsT=lhs, lhsT_scale=lhs_scale, rhs=rhs, rhs_scale=rhs_scale,
+                                    start=(side == 0), stop=(side == 1))
+            return acc
+
+        acc = {}
+        for t in range(PACK):
+            acc["a", t] = product("bank_a%d" % t, t, 0)
+            acc["b", t] = product("bank_b%d" % t, t, 1)
+        board = {}
+        for t in range(PACK):
+            board["a", t] = board_a[t]
+            board["b", t] = board_b[t]
+        places = {"a": list3, "b": list4}
+
+        def on_vector(dst, src):
+            nc.vector.tensor_copy(dst, src)
+
+        def on_scalar(dst, src):
+            nc.scalar.activation(dst, src, COPY)
+
+        staged = {}
+
+        def stage(copy, which, t):
+            staged[which, t] = tile("%s%d" % (which, t), [P, J], F32)
+            copy(staged[which, t][:], acc[which, t][:])
+
+        def place(copy, which, t):
+            copy(board[which, t][:].indirect(places[which][:]), staged[which, t][:])
+
+        def place_half(copy, which, t, half):
+            copy(board[which, t][:].indirect(places[which][:, 8 * half : 8 * half + 8]),
+                 staged[which, t][:, P * half : P * half + P])
+
+        hid = tile("hid", [P, O, PACK], BF16)
+        total = {}
+
+        def join(engine, t):
+            total[t] = tile("board%d" % t, [P, C], F32)
+            engine.tensor_tensor(total[t][:], board_a[t][:], board_b[t][:], ADD)
+
+        def read(t):
+            nc.vector.tensor_copy(hid[:, :, t], total[t][:].indirect(list5[:]))
+
+        stage(on_scalar, "a", 0)
+        stage(on_scalar, "b", 0)
+        place(on_vector, "a", 0)
+        stage(on_scalar, "b", 1)
+        place(on_scalar, "b", 0)
+        stage(on_vector, "a", 1)
+        stage(on_vector, "a", 3)
+        stage(on_scalar, "a", 2)
+        place(on_vector, "a", 1)
+        place(on_scalar, "b", 1)
+        stage(on_scalar, "b", 2)
+        join(nc.vector, 0)
+        join(nc.vector, 1)
+        read(0)
+        place(on_scalar, "a", 2)
+        read(1)
+        stage(on_scalar, "b", 3)
+        place(on_vector, "a", 3)
+        place(on_scalar, "b", 2)
+        place(on_scalar, "b", 3)
+        join(nc.vector, 2)
+        read(2)
+        join(nc.vector, 3)
+        read(3)
+
+        hid_codes = tile("hid_codes", [P, O], U32)
+        hid_plane = tile("hid_plane", [P, O], U8)
+        nc.vector.quantize_mx(out=hid_codes[:].bitcast(E5M2), scales=hid_plane[:],
+                              in_=hid[:].rearrange("p o t -> p (o t)"))
+
+        for h, copy, queue in ((0, on_scalar, nc.scalar), (1, on_vector, nc.sync)):
+            sums = psum.tile([P, O], F32, name="bank_a%d" % h)
+            nc.tensor.matmul_mx(out=sums[:], lhsT=wb_codes[:, 2 * P * h : 2 * P * (h + 1)].bitcast(E2M1),
+                                lhsT_scale=wb_plane[:, P * h : P * (h + 1)],
+                                rhs=hid_codes[:].bitcast(E5M2), rhs_scale=hid_plane[:], start=True, stop=True)
+            whole = tile("p%d" % h, [P, O], F32)
+            copy(whole[:], sums[:])
+            first = tile("first%d" % h, [P, E], F32)
+            second = tile("second%d" % h, [P, E], F32)
+            copy(first[:], whole[:].indirect(list6[:]))
+            copy(second[:], whole[:].indirect(list7[:]))
+            larger = tile("larger%d" % h, [P, E], F32)
+            nc.vector.tensor_tensor(larger[:], first[:], second[:], MAX)
+            queue.dma_start(out=out[P * h : P * (h + 1), :], in_=larger[:])

@@ -67,24 +67,25 @@ def tile_list_crossed_shared_one_bestoftwo_kernel(
         xo_plane = tile("xo_plane", [P, Z], U8)
         w_planes = tile("w_planes", [P, 2 * R], U8)
         wb_plane = tile("wb_plane", [P, N], U8)
-        for plane in (xt_plane, xo_plane, wb_plane):
-            nc.vector.memset(plane[:].bitcast(I32), 0)
         load_scales_everywhere(nc.gpsimd, w_planes[:, 0:R], w_scales)
         load_scales_everywhere(nc.gpsimd, w_planes[:, R : 2 * R], w2_scales)
-        board_a = [tile("board_a%d" % t, [P, C], F32) for t in range(PACK)]
-        board_b = [tile("board_b%d" % t, [P, C], F32) for t in range(PACK)]
-        for t in range(PACK):
-            nc.gpsimd.memset(board_a[t][:], 0.0)
-            nc.gpsimd.memset(board_b[t][:], 0.0)
+        for plane in (xt_plane, xo_plane, wb_plane):
+            nc.vector.memset(plane[:].bitcast(I32), 0)
+        board_a = [tile("board_a%d" % u, [P, C], F32) for u in range(2)]
+        board_b = [tile("board_b%d" % u, [P, C], F32) for u in range(2)]
+        for u in range(2):
+            for fresh in (board_a[u], board_b[u]):
+                nc.vector.memset(fresh[:, 0 : C - 1], 0.0)
+                nc.vector.memset(fresh[:, C - 1 : C], 0.0)
 
         list1 = load_list("list1", offs)
-        w_codes = load_words(nc.scalar, "w_codes", w_words[0].rearrange("p n t -> p (n t)"), [P, R], U32)
-        w2_codes = load_words(nc.scalar, "w2_codes", w2_words[0].rearrange("p n t -> p (n t)"), [P, R], U32)
         xt_codes = load_words(nc.scalar, "xt_codes", xt_words[0], [P, T], U16)
-        xo_codes = load_words(nc.scalar, "xo_codes", xo_words[0].rearrange("p n t -> p (n t)"), [P, Z], U32)
         list2 = load_list("list2", offs2)
+        w_codes = load_words(nc.sync, "w_codes", w_words[0].rearrange("p n t -> p (n t)"), [P, R], U32)
+        xo_codes = load_words(nc.scalar, "xo_codes", xo_words[0].rearrange("p n t -> p (n t)"), [P, Z], U32)
         load_scales(nc.sync, xt_plane[:], xt_scales)
         load_scales(nc.sync, xo_plane[:], xo_scales)
+        w2_codes = load_words(nc.sync, "w2_codes", w2_words[0].rearrange("p n t -> p (n t)"), [P, R], U32)
         list3 = load_list("list3", offs3)
         list4 = load_list("list4", offs4)
         list5 = load_list("list5", offs5)
@@ -105,47 +106,46 @@ def tile_list_crossed_shared_one_bestoftwo_kernel(
         xt_pick_s = tile("xt_pick_s", [P, J], U8)
         xo_pick = tile("xo_pick", [P, J], U32)
         xo_pick_s = tile("xo_pick_s", [P, J], U8)
-        nc.vector.tensor_copy(xt_pick_s[:], xt_plane[:].indirect(list1[:]))
         nc.vector.tensor_copy(xt_pick[:], xt_codes[:].indirect(list1[:]))
+        nc.vector.tensor_copy(xt_pick_s[:], xt_plane[:].indirect(list1[:]))
         nc.vector.tensor_copy(xo_pick_s[:], xo_plane[:].indirect(list2[:]))
         nc.vector.tensor_copy(xo_pick[:], xo_codes[:].indirect(list2[:]))
 
-        by_slot = w_planes[:].rearrange("p (c i t) -> p c t i", t=PACK, i=16)
-        planes_first = tile("planes_first", [P, 2 * P], U8)
-        planes_rest = tile("planes_rest", [P, (PACK - 1) * 2 * P], U8)
-        nc.vector.tensor_copy(planes_first[:].rearrange("p (c i) -> p c i", i=16), by_slot[:, :, 0, :])
-        nc.vector.tensor_copy(
-            planes_rest[:].rearrange("p (t c i) -> p c t i", t=PACK - 1, i=16), by_slot[:, :, 1:PACK, :]
-        )
+        planes_dealt = []
+        for t in range(PACK):
+            dealt = tile("planes_dealt%d" % t, [P, 2 * P], U8)
+            nc.gpsimd.tensor_copy(dealt[:], w_planes[:].rearrange("p (m t) -> p m t", t=PACK)[:, :, t])
+            planes_dealt.append(dealt)
 
         def weight(which, t):
             codes, fmt = ((w_dealt, E4M3), (w2_dealt, E5M2))[which]
-            if t == 0:
-                plane = planes_first[:, which * P : (which + 1) * P]
-            else:
-                start = (2 * (t - 1) + which) * P
-                plane = planes_rest[:, start : start + P]
+            plane = planes_dealt[t][:, which * P : (which + 1) * P]
             return codes[:, t * P : (t + 1) * P].bitcast(fmt), plane
 
         moving = ((xt_pick[:].bitcast(E2M1), xt_pick_s[:]), (xo_pick[:].bitcast(E4M3), xo_pick_s[:]))
 
         def product(name, t, crossed):
             acc = psum.tile([P, J], F32, name=name)
-            for side in range(2):
-                lhs, lhs_scale = weight(side ^ crossed, t)
-                rhs, rhs_scale = moving[side]
+            for which in (1, 0):
+                lhs, lhs_scale = weight(which, t)
+                rhs, rhs_scale = moving[which ^ crossed]
                 nc.tensor.matmul_mx(out=acc[:], lhsT=lhs, lhsT_scale=lhs_scale, rhs=rhs, rhs_scale=rhs_scale,
-                                    start=(side == 0), stop=(side == 1))
+                                    start=(which == 1), stop=(which == 0))
             return acc
 
+        order = [("a", 0), ("b", 0), ("b", 1), ("a", 1), ("a", 2), ("b", 2), ("a", 3), ("b", 3)]
         acc = {}
-        for t in range(PACK):
-            acc["a", t] = product("bank_a%d" % t, t, 0)
-            acc["b", t] = product("bank_b%d" % t, t, 1)
+
+        def multiply(step):
+            which, t = order[step]
+            acc[which, t] = product("bank%d" % (step % 3), t, int(which == "b"))
+
+        for step in range(3):
+            multiply(step)
         board = {}
         for t in range(PACK):
-            board["a", t] = board_a[t]
-            board["b", t] = board_b[t]
+            board["a", t] = board_a[t % 2]
+            board["b", t] = board_b[t % 2]
         places = {"a": list3, "b": list4}
 
         def on_vector(dst, src):
@@ -159,6 +159,9 @@ def tile_list_crossed_shared_one_bestoftwo_kernel(
         def stage(copy, which, t):
             staged[which, t] = tile("%s%d" % (which, t), [P, J], F32)
             copy(staged[which, t][:], acc[which, t][:])
+            step = order.index((which, t)) + 3
+            if step < len(order):
+                multiply(step)
 
         def place(copy, which, t):
             copy(board[which, t][:].indirect(places[which][:]), staged[which, t][:])
@@ -172,10 +175,14 @@ def tile_list_crossed_shared_one_bestoftwo_kernel(
 
         def join(engine, t):
             total[t] = tile("board%d" % t, [P, C], F32)
-            engine.tensor_tensor(total[t][:], board_a[t][:], board_b[t][:], ADD)
+            engine.tensor_tensor(total[t][:], board["a", t][:], board["b", t][:], ADD)
 
         def read(t):
-            nc.vector.tensor_copy(hid[:, :, t], total[t][:].indirect(list5[:]))
+            if t < PACK - 1:
+                nc.vector.tensor_copy(hid[:, :, t], total[t][:].indirect(list5[:]))
+            else:
+                for u in range(2):
+                    nc.vector.tensor_copy(hid[:, P * u : P * (u + 1), t], total[t][:].indirect(list5[:, 8 * u : 8 * u + 8]))
 
         stage(on_scalar, "a", 0)
         stage(on_scalar, "b", 0)
@@ -183,37 +190,40 @@ def tile_list_crossed_shared_one_bestoftwo_kernel(
         stage(on_scalar, "b", 1)
         place(on_scalar, "b", 0)
         stage(on_vector, "a", 1)
-        stage(on_vector, "a", 3)
         stage(on_scalar, "a", 2)
+        join(nc.vector, 0)
         place(on_vector, "a", 1)
         place(on_scalar, "b", 1)
+        stage(on_scalar, "a", 3)
         stage(on_scalar, "b", 2)
-        join(nc.vector, 0)
-        join(nc.vector, 1)
         read(0)
+        join(nc.vector, 1)
         place(on_scalar, "a", 2)
-        read(1)
         stage(on_scalar, "b", 3)
         place(on_vector, "a", 3)
         place(on_scalar, "b", 2)
+        read(1)
         place(on_scalar, "b", 3)
         join(nc.vector, 2)
         read(2)
         join(nc.vector, 3)
         read(3)
 
-        hid_codes = tile("hid_codes", [P, O], U32)
-        hid_plane = tile("hid_plane", [P, O], U8)
-        nc.vector.quantize_mx(out=hid_codes[:].bitcast(E5M2), scales=hid_plane[:],
-                              in_=hid[:].rearrange("p o t -> p (o t)"))
+        sums = [psum.tile([P, O], F32, name="sums%d" % h) for h in range(2)]
+        for u in range(2):
+            hid_codes = tile("hid_codes%d" % u, [P, P], U32)
+            hid_plane = tile("hid_plane%d" % u, [P, P], U8)
+            nc.vector.quantize_mx(out=hid_codes[:].bitcast(E5M2), scales=hid_plane[:],
+                                  in_=hid[:, P * u : P * (u + 1), :].rearrange("p o t -> p (o t)"))
+            for h in range(2):
+                nc.tensor.matmul_mx(out=sums[h][:, P * u : P * (u + 1)],
+                                    lhsT=wb_codes[:, 2 * P * h : 2 * P * (h + 1)].bitcast(E2M1),
+                                    lhsT_scale=wb_plane[:, P * h : P * (h + 1)],
+                                    rhs=hid_codes[:].bitcast(E5M2), rhs_scale=hid_plane[:], start=True, stop=True)
 
         for h, copy, queue in ((0, on_scalar, nc.scalar), (1, on_vector, nc.sync)):
-            sums = psum.tile([P, O], F32, name="bank_a%d" % h)
-            nc.tensor.matmul_mx(out=sums[:], lhsT=wb_codes[:, 2 * P * h : 2 * P * (h + 1)].bitcast(E2M1),
-                                lhsT_scale=wb_plane[:, P * h : P * (h + 1)],
-                                rhs=hid_codes[:].bitcast(E5M2), rhs_scale=hid_plane[:], start=True, stop=True)
             whole = tile("p%d" % h, [P, O], F32)
-            copy(whole[:], sums[:])
+            copy(whole[:], sums[h][:])
             first = tile("first%d" % h, [P, E], F32)
             second = tile("second%d" % h, [P, E], F32)
             copy(first[:], whole[:].indirect(list6[:]))

@@ -67,16 +67,14 @@ def tile_list_crossed_shared_one_bestoftwo_kernel(
         xo_plane = tile("xo_plane", [P, Z], U8)
         w_planes = tile("w_planes", [P, 2 * R], U8)
         wb_plane = tile("wb_plane", [P, N], U8)
-        load_scales_everywhere(nc.gpsimd, w_planes[:, 0:R], w_scales)
         load_scales_everywhere(nc.gpsimd, w_planes[:, R : 2 * R], w2_scales)
-        for plane in (xt_plane, xo_plane, wb_plane):
-            nc.vector.memset(plane[:].bitcast(I32), 0)
+        for plane in (xt_plane[:], xo_plane[:], w_planes[:, 0:R], wb_plane[:]):
+            nc.vector.memset(plane.bitcast(I32), 0)
         board_a = [tile("board_a%d" % u, [P, C], F32) for u in range(2)]
         board_b = [tile("board_b%d" % u, [P, C], F32) for u in range(2)]
-        for u in range(2):
-            for fresh in (board_a[u], board_b[u]):
-                nc.vector.memset(fresh[:, 0 : C - 1], 0.0)
-                nc.vector.memset(fresh[:, C - 1 : C], 0.0)
+        for u, engine in enumerate((nc.vector, nc.gpsimd)):
+            engine.memset(board_a[u][:], 0.0)
+            engine.memset(board_b[u][:], 0.0)
 
         list1 = load_list("list1", offs)
         xt_codes = load_words(nc.scalar, "xt_codes", xt_words[0], [P, T], U16)
@@ -86,6 +84,7 @@ def tile_list_crossed_shared_one_bestoftwo_kernel(
         load_scales(nc.sync, xt_plane[:], xt_scales)
         load_scales(nc.sync, xo_plane[:], xo_scales)
         w2_codes = load_words(nc.sync, "w2_codes", w2_words[0].rearrange("p n t -> p (n t)"), [P, R], U32)
+        load_scales(nc.sync, w_planes[:, 0:R], w_scales)
         list3 = load_list("list3", offs3)
         list4 = load_list("list4", offs4)
         list5 = load_list("list5", offs5)
@@ -111,11 +110,14 @@ def tile_list_crossed_shared_one_bestoftwo_kernel(
         nc.vector.tensor_copy(xo_pick_s[:], xo_plane[:].indirect(list2[:]))
         nc.vector.tensor_copy(xo_pick[:], xo_codes[:].indirect(list2[:]))
 
-        planes_dealt = []
-        for t in range(PACK):
-            dealt = tile("planes_dealt%d" % t, [P, 2 * P], U8)
-            nc.gpsimd.tensor_copy(dealt[:], w_planes[:].rearrange("p (m t) -> p m t", t=PACK)[:, :, t])
-            planes_dealt.append(dealt)
+        by_slot = w_planes[:].rearrange("p (c i t) -> p c t i", t=PACK, i=16)
+        planes_first = tile("planes_first", [P, 2 * P], U8)
+        planes_rest = tile("planes_rest", [P, (PACK - 1) * 2 * P], U8)
+        nc.vector.tensor_copy(planes_first[:].rearrange("p (c i) -> p c i", i=16), by_slot[:, :, 0, :])
+        nc.vector.tensor_copy(
+            planes_rest[:].rearrange("p (t c i) -> p c t i", t=PACK - 1, i=16), by_slot[:, :, 1:PACK, :]
+        )
+        planes_dealt = [planes_first[:]] + [planes_rest[:, 2 * P * t : 2 * P * (t + 1)] for t in range(PACK - 1)]
 
         def weight(which, t):
             codes, fmt = ((w_dealt, E4M3), (w2_dealt, E5M2))[which]
@@ -209,25 +211,25 @@ def tile_list_crossed_shared_one_bestoftwo_kernel(
         join(nc.vector, 3)
         read(3)
 
-        sums = [psum.tile([P, O], F32, name="sums%d" % h) for h in range(2)]
+        whole = [tile("p%d" % h, [P, O], F32) for h in range(2)]
         for u in range(2):
             hid_codes = tile("hid_codes%d" % u, [P, P], U32)
             hid_plane = tile("hid_plane%d" % u, [P, P], U8)
             nc.vector.quantize_mx(out=hid_codes[:].bitcast(E5M2), scales=hid_plane[:],
                                   in_=hid[:, P * u : P * (u + 1), :].rearrange("p o t -> p (o t)"))
             for h in range(2):
-                nc.tensor.matmul_mx(out=sums[h][:, P * u : P * (u + 1)],
-                                    lhsT=wb_codes[:, 2 * P * h : 2 * P * (h + 1)].bitcast(E2M1),
+                sums = psum.tile([P, P], F32, name="sums%d%d" % (h, u))
+                nc.tensor.matmul_mx(out=sums[:], lhsT=wb_codes[:, 2 * P * h : 2 * P * (h + 1)].bitcast(E2M1),
                                     lhsT_scale=wb_plane[:, P * h : P * (h + 1)],
                                     rhs=hid_codes[:].bitcast(E5M2), rhs_scale=hid_plane[:], start=True, stop=True)
+                on_scalar(whole[h][:, P * u : P * (u + 1)], sums[:])
 
-        for h, copy, queue in ((0, on_scalar, nc.scalar), (1, on_vector, nc.sync)):
-            whole = tile("p%d" % h, [P, O], F32)
-            copy(whole[:], sums[h][:])
-            first = tile("first%d" % h, [P, E], F32)
-            second = tile("second%d" % h, [P, E], F32)
-            copy(first[:], whole[:].indirect(list6[:]))
-            copy(second[:], whole[:].indirect(list7[:]))
+        first = [tile("first%d" % h, [P, E], F32) for h in range(2)]
+        second = [tile("second%d" % h, [P, E], F32) for h in range(2)]
+        for h in range(2):
+            on_vector(first[h][:], whole[h][:].indirect(list6[:]))
+            on_scalar(second[h][:], whole[h][:].indirect(list7[:]))
+        for h, queue in ((0, nc.sync), (1, nc.scalar)):
             larger = tile("larger%d" % h, [P, E], F32)
-            nc.vector.tensor_tensor(larger[:], first[:], second[:], MAX)
+            nc.vector.tensor_tensor(larger[:], first[h][:], second[h][:], MAX)
             queue.dma_start(out=out[P * h : P * (h + 1), :], in_=larger[:])

@@ -135,7 +135,7 @@ def tile_list_crossed_shared_one_bestoftwo_kernel(
                                     start=(which == 1), stop=(which == 0))
             return acc
 
-        order = [("a", 0), ("b", 0), ("b", 1), ("a", 1), ("a", 2), ("b", 2), ("a", 3), ("b", 3)]
+        order = [("a", 0), ("b", 0), ("b", 1), ("a", 1), ("b", 2), ("a", 2), ("a", 3), ("b", 3)]
         acc = {}
 
         def multiply(step):
@@ -192,21 +192,21 @@ def tile_list_crossed_shared_one_bestoftwo_kernel(
         stage(on_scalar, "b", 1)
         place(on_scalar, "b", 0)
         stage(on_vector, "a", 1)
-        stage(on_scalar, "a", 2)
-        join(nc.vector, 0)
+        stage(on_vector, "b", 2)
+        join(nc.gpsimd, 0)
         place(on_vector, "a", 1)
         place(on_scalar, "b", 1)
-        stage(on_scalar, "a", 3)
-        stage(on_scalar, "b", 2)
-        read(0)
-        join(nc.vector, 1)
-        place(on_scalar, "a", 2)
-        stage(on_scalar, "b", 3)
-        place(on_vector, "a", 3)
+        stage(on_vector, "a", 2)
+        stage(on_vector, "a", 3)
+        join(nc.gpsimd, 1)
         place(on_scalar, "b", 2)
+        place(on_vector, "a", 2)
+        stage(on_scalar, "b", 3)
+        join(nc.gpsimd, 2)
+        place(on_scalar, "a", 3)
+        read(0)
         read(1)
         place(on_scalar, "b", 3)
-        join(nc.vector, 2)
         read(2)
         join(nc.vector, 3)
         read(3)

@@ -19,26 +19,20 @@ ADD = mybir.AluOpType.add
 MAX = mybir.AluOpType.max
 
 P = 128
-PACK = 4
+SLOTS = 4
+LINE = 16
+ENTRIES = 16
+BANKS = 3
 PERIOD = 14
+REPEATS = 5
 
 
-def repeated(rows, times):
-    return rows.unsqueeze(0).to_broadcast([times, rows.shape[0], rows.shape[1]])
-
-
-def load_scales(queue, plane, scales):
+def load_scales(first_queue, last_queue, plane, scales):
     rows = scales[0].bitcast(I32)
     words = plane.bitcast(I32)
-    queue.dma_start(out=words[0 : PERIOD * 5, :], in_=repeated(rows[0:PERIOD, :], 5))
-    queue.dma_start(out=words[96:100, :], in_=rows[12:16, :])
-
-
-def load_scales_everywhere(queue, plane, scales):
-    rows = scales[0].bitcast(I32)
-    words = plane.bitcast(I32)
-    queue.dma_start(out=words[0 : PERIOD * 7, :], in_=repeated(rows[0:PERIOD, :], 7))
-    queue.dma_start(out=words[PERIOD * 7 : P, :], in_=repeated(rows[PERIOD:16, :], 15))
+    repeated = rows[0:PERIOD, :].unsqueeze(0).to_broadcast([REPEATS, PERIOD, rows.shape[1]])
+    first_queue.dma_start(out=words[0 : PERIOD * REPEATS, :], in_=repeated)
+    last_queue.dma_start(out=words[96:100, :], in_=rows[12:16, :])
 
 
 def tile_list_crossed_shared_one_bestoftwo_kernel(
@@ -50,8 +44,8 @@ def tile_list_crossed_shared_one_bestoftwo_kernel(
         keep = ctx.enter_context(tc.tile_pool(name="keep", bufs=1))
         psum = ctx.enter_context(tc.psum_pool(name="psum", bufs=1))
 
-        def tile(name, shape, dtype):
-            return keep.tile(shape, dtype, name=name, align_bytes=64)
+        def tile(name, shape, dtype, tag=None):
+            return keep.tile(shape, dtype, name=name, tag=tag or name, align_bytes=64)
 
         def load_list(name, source):
             held = keep.tile(list(source.shape), U16, name=name)
@@ -63,92 +57,88 @@ def tile_list_crossed_shared_one_bestoftwo_kernel(
             queue.dma_start(out=held[:].bitcast(I32), in_=source.bitcast(I32))
             return held
 
+        def flat(words):
+            return words[0].rearrange("p n t -> p (n t)")
+
+        def deal(copy, name, source, dtype, run):
+            width = source.shape[1] // SLOTS
+            by_slot = source.rearrange("p (c i t) -> p c t i", t=SLOTS, i=run)
+            first_slot = tile(name + "_first", [P, width], dtype)
+            other_slots = tile(name + "_rest", [P, (SLOTS - 1) * width], dtype)
+            copy(first_slot[:].rearrange("p (c i) -> p c i", i=run), by_slot[:, :, 0, :])
+            copy(other_slots[:].rearrange("p (t c i) -> p c t i", t=SLOTS - 1, i=run), by_slot[:, :, 1:SLOTS, :])
+            return [first_slot[:]] + [other_slots[:, width * t : width * (t + 1)] for t in range(SLOTS - 1)]
+
         xt_plane = tile("xt_plane", [P, T], U8)
         xo_plane = tile("xo_plane", [P, Z], U8)
         w_planes = tile("w_planes", [P, 2 * R], U8)
         wb_plane = tile("wb_plane", [P, N], U8)
-        load_scales_everywhere(nc.gpsimd, w_planes[:, R : 2 * R], w2_scales)
-        for plane in (xt_plane[:], xo_plane[:], w_planes[:, 0:R], wb_plane[:]):
-            nc.vector.memset(plane.bitcast(I32), 0)
-        board_a = [tile("board_a%d" % u, [P, C], F32) for u in range(2)]
-        board_b = [tile("board_b%d" % u, [P, C], F32) for u in range(2)]
-        for u, engine in enumerate((nc.vector, nc.gpsimd)):
-            engine.memset(board_a[u][:], 0.0)
-            engine.memset(board_b[u][:], 0.0)
+        nc.gpsimd.memset(w_planes[:].bitcast(I32), 0)
+        for plane in (xt_plane, xo_plane, wb_plane):
+            nc.vector.memset(plane[:].bitcast(I32), 0)
 
-        list1 = load_list("list1", offs)
+        token_list = load_list("token_list", offs)
         xt_codes = load_words(nc.scalar, "xt_codes", xt_words[0], [P, T], U16)
-        list2 = load_list("list2", offs2)
-        w_codes = load_words(nc.sync, "w_codes", w_words[0].rearrange("p n t -> p (n t)"), [P, R], U32)
-        xo_codes = load_words(nc.scalar, "xo_codes", xo_words[0].rearrange("p n t -> p (n t)"), [P, Z], U32)
-        load_scales(nc.sync, xt_plane[:], xt_scales)
-        load_scales(nc.sync, xo_plane[:], xo_scales)
-        w2_codes = load_words(nc.sync, "w2_codes", w2_words[0].rearrange("p n t -> p (n t)"), [P, R], U32)
-        load_scales(nc.sync, w_planes[:, 0:R], w_scales)
-        list3 = load_list("list3", offs3)
-        list4 = load_list("list4", offs4)
-        list5 = load_list("list5", offs5)
+        note_list = load_list("note_list", offs2)
+        w_codes = load_words(nc.sync, "w_codes", flat(w_words), [P, R], U32)
+        xo_codes = load_words(nc.scalar, "xo_codes", flat(xo_words), [P, Z], U32)
+        load_scales(nc.sync, nc.sync, xt_plane[:], xt_scales)
+        load_scales(nc.sync, nc.sync, xo_plane[:], xo_scales)
+        w2_codes = load_words(nc.sync, "w2_codes", flat(w2_words), [P, R], U32)
+        load_scales(nc.gpsimd, nc.sync, w_planes[:, 0:R], w_scales)
+        load_scales(nc.gpsimd, nc.sync, w_planes[:, R : 2 * R], w2_scales)
+        places = {"a": load_list("a_places", offs3), "b": load_list("b_places", offs4)}
+        read_list = load_list("read_list", offs5)
         wb_codes = load_words(nc.sync, "wb_codes", wb_words[0], [P, 2 * N], U8)
-        load_scales(nc.sync, wb_plane[:], wb_scales)
-        list6 = load_list("list6", offs6)
-        list7 = load_list("list7", offs7)
+        load_scales(nc.sync, nc.sync, wb_plane[:], wb_scales)
+        first_list = load_list("first_list", offs6)
+        second_list = load_list("second_list", offs7)
 
-        w_dealt = tile("w_dealt", [P, R], U32)
-        w2_dealt = tile("w2_dealt", [P, R], U32)
-        for dealt, codes in ((w_dealt, w_codes), (w2_dealt, w2_codes)):
-            nc.scalar.copy(
-                dealt[:].rearrange("p (t c i) -> p c t i", t=PACK, i=4),
-                codes[:].rearrange("p (c i t) -> p c t i", t=PACK, i=4),
-            )
+        boards = {"a": [tile("board_a0", [P, C], F32)], "b": [tile("board_b0", [P, C], F32)]}
+        nc.vector.memset(boards["a"][0][:], 0.0)
+        nc.vector.memset(boards["b"][0][:], 0.0)
 
-        xt_pick = tile("xt_pick", [P, J], U16)
-        xt_pick_s = tile("xt_pick_s", [P, J], U8)
-        xo_pick = tile("xo_pick", [P, J], U32)
-        xo_pick_s = tile("xo_pick_s", [P, J], U8)
-        nc.vector.tensor_copy(xt_pick[:], xt_codes[:].indirect(list1[:]))
-        nc.vector.tensor_copy(xt_pick_s[:], xt_plane[:].indirect(list1[:]))
-        nc.vector.tensor_copy(xo_pick_s[:], xo_plane[:].indirect(list2[:]))
-        nc.vector.tensor_copy(xo_pick[:], xo_codes[:].indirect(list2[:]))
+        words_dealt = [
+            deal(nc.scalar.copy, name, codes[:], U32, LINE // 4) for name, codes in (("w", w_codes), ("w2", w2_codes))
+        ]
 
-        by_slot = w_planes[:].rearrange("p (c i t) -> p c t i", t=PACK, i=16)
-        planes_first = tile("planes_first", [P, 2 * P], U8)
-        planes_rest = tile("planes_rest", [P, (PACK - 1) * 2 * P], U8)
-        nc.vector.tensor_copy(planes_first[:].rearrange("p (c i) -> p c i", i=16), by_slot[:, :, 0, :])
-        nc.vector.tensor_copy(
-            planes_rest[:].rearrange("p (t c i) -> p c t i", t=PACK - 1, i=16), by_slot[:, :, 1:PACK, :]
-        )
-        planes_dealt = [planes_first[:]] + [planes_rest[:, 2 * P * t : 2 * P * (t + 1)] for t in range(PACK - 1)]
+        boards["b"].append(tile("board_b1", [P, C], F32, tag="w_codes"))
+        boards["a"].append(tile("board_a1", [P, C], F32, tag="w2_codes"))
+        nc.gpsimd.memset(boards["b"][1][:], 0.0)
+        nc.gpsimd.memset(boards["a"][1][:], 0.0)
 
-        def weight(which, t):
-            codes, fmt = ((w_dealt, E4M3), (w2_dealt, E5M2))[which]
-            plane = planes_dealt[t][:, which * P : (which + 1) * P]
-            return codes[:, t * P : (t + 1) * P].bitcast(fmt), plane
+        xt_picked = tile("xt_picked", [P, J], U16)
+        xt_picked_plane = tile("xt_picked_plane", [P, J], U8)
+        nc.vector.tensor_copy(xt_picked[:], xt_codes[:].indirect(token_list[:]))
+        nc.vector.tensor_copy(xt_picked_plane[:], xt_plane[:].indirect(token_list[:]))
+        xo_picked = tile("xo_picked", [P, J], U32, tag="xt_plane")
+        xo_picked_plane = tile("xo_picked_plane", [P, J], U8)
+        nc.vector.tensor_copy(xo_picked_plane[:], xo_plane[:].indirect(note_list[:]))
+        nc.vector.tensor_copy(xo_picked[:], xo_codes[:].indirect(note_list[:]))
+        tokens = (xt_picked[:].bitcast(E2M1), xt_picked_plane[:])
+        notes = (xo_picked[:].bitcast(E4M3), xo_picked_plane[:])
 
-        moving = ((xt_pick[:].bitcast(E2M1), xt_pick_s[:]), (xo_pick[:].bitcast(E4M3), xo_pick_s[:]))
+        planes_dealt = deal(nc.vector.tensor_copy, "planes", w_planes[:], U8, LINE)
 
-        def product(name, t, crossed):
-            acc = psum.tile([P, J], F32, name=name)
-            for which in (1, 0):
-                lhs, lhs_scale = weight(which, t)
-                rhs, rhs_scale = moving[which ^ crossed]
-                nc.tensor.matmul_mx(out=acc[:], lhsT=lhs, lhsT_scale=lhs_scale, rhs=rhs, rhs_scale=rhs_scale,
-                                    start=(which == 1), stop=(which == 0))
-            return acc
-
-        order = [("a", 0), ("b", 0), ("b", 1), ("a", 1), ("b", 2), ("a", 2), ("a", 3), ("b", 3)]
-        acc = {}
+        results = [("a", 0), ("b", 0), ("b", 1), ("a", 1), ("b", 2), ("a", 2), ("a", 3), ("b", 3)]
+        partner = {"a": (tokens, notes), "b": (notes, tokens)}
+        sums = {}
 
         def multiply(step):
-            which, t = order[step]
-            acc[which, t] = product("bank%d" % (step % 3), t, int(which == "b"))
-
-        for step in range(3):
-            multiply(step)
-        board = {}
-        for t in range(PACK):
-            board["a", t] = board_a[t % 2]
-            board["b", t] = board_b[t % 2]
-        places = {"a": list3, "b": list4}
+            result, t = results[step]
+            bank = psum.tile([P, J], F32, name="bank%d" % (step % BANKS))
+            for matrix, fmt in ((1, E5M2), (0, E4M3)):
+                codes, plane = partner[result][matrix]
+                nc.tensor.matmul_mx(
+                    out=bank[:],
+                    lhsT=words_dealt[matrix][t].bitcast(fmt),
+                    lhsT_scale=planes_dealt[t][:, matrix * P : (matrix + 1) * P],
+                    rhs=codes,
+                    rhs_scale=plane,
+                    start=(matrix == 1),
+                    stop=(matrix == 0),
+                )
+            sums[result, t] = bank
 
         def on_vector(dst, src):
             nc.vector.tensor_copy(dst, src)
@@ -157,34 +147,29 @@ def tile_list_crossed_shared_one_bestoftwo_kernel(
             nc.scalar.activation(dst, src, COPY)
 
         staged = {}
+        joined = {}
+        hid = tile("hid", [P, O, SLOTS], BF16)
+        half_list = P // ENTRIES
 
-        def stage(copy, which, t):
-            staged[which, t] = tile("%s%d" % (which, t), [P, J], F32)
-            copy(staged[which, t][:], acc[which, t][:])
-            step = order.index((which, t)) + 3
-            if step < len(order):
+        def stage(copy, result, t):
+            staged[result, t] = tile("%s%d" % (result, t), [P, J], F32)
+            copy(staged[result, t][:], sums[result, t][:])
+            step = results.index((result, t)) + BANKS
+            if step < len(results):
                 multiply(step)
 
-        def place(copy, which, t):
-            copy(board[which, t][:].indirect(places[which][:]), staged[which, t][:])
-
-        def place_half(copy, which, t, half):
-            copy(board[which, t][:].indirect(places[which][:, 8 * half : 8 * half + 8]),
-                 staged[which, t][:, P * half : P * half + P])
-
-        hid = tile("hid", [P, O, PACK], BF16)
-        total = {}
+        def place(copy, result, t):
+            copy(boards[result][t % 2][:].indirect(places[result][:]), staged[result, t][:])
 
         def join(engine, t):
-            total[t] = tile("board%d" % t, [P, C], F32)
-            engine.tensor_tensor(total[t][:], board["a", t][:], board["b", t][:], ADD)
+            joined[t] = tile("pg%d" % t, [P, C], F32)
+            engine.tensor_tensor(joined[t][:], boards["a"][t % 2][:], boards["b"][t % 2][:], ADD)
 
         def read(t):
-            if t < PACK - 1:
-                nc.vector.tensor_copy(hid[:, :, t], total[t][:].indirect(list5[:]))
-            else:
-                for u in range(2):
-                    nc.vector.tensor_copy(hid[:, P * u : P * (u + 1), t], total[t][:].indirect(list5[:, 8 * u : 8 * u + 8]))
+            nc.vector.tensor_copy(hid[:, :, t], joined[t][:].indirect(read_list[:]))
+
+        for step in range(BANKS):
+            multiply(step)
 
         stage(on_scalar, "a", 0)
         stage(on_scalar, "b", 0)
@@ -208,28 +193,41 @@ def tile_list_crossed_shared_one_bestoftwo_kernel(
         read(1)
         place(on_scalar, "b", 3)
         read(2)
-        join(nc.vector, 3)
-        read(3)
+        last = SLOTS - 1
+        join(nc.vector, last)
 
-        whole = [tile("p%d" % h, [P, O], F32) for h in range(2)]
+        for u in range(2):
+            picked = joined[last][:].indirect(read_list[:, half_list * u : half_list * (u + 1)])
+            nc.vector.tensor_copy(hid[:, P * u : P * (u + 1), last], picked)
+
+        p_rows = [tile("p%d" % h, [P, O], F32) for h in range(N // P)]
         for u in range(2):
             hid_codes = tile("hid_codes%d" % u, [P, P], U32)
             hid_plane = tile("hid_plane%d" % u, [P, P], U8)
-            nc.vector.quantize_mx(out=hid_codes[:].bitcast(E5M2), scales=hid_plane[:],
-                                  in_=hid[:, P * u : P * (u + 1), :].rearrange("p o t -> p (o t)"))
-            for h in range(2):
-                sums = psum.tile([P, P], F32, name="sums%d%d" % (h, u))
-                nc.tensor.matmul_mx(out=sums[:], lhsT=wb_codes[:, 2 * P * h : 2 * P * (h + 1)].bitcast(E2M1),
-                                    lhsT_scale=wb_plane[:, P * h : P * (h + 1)],
-                                    rhs=hid_codes[:].bitcast(E5M2), rhs_scale=hid_plane[:], start=True, stop=True)
-                on_scalar(whole[h][:, P * u : P * (u + 1)], sums[:])
+            nc.vector.quantize_mx(
+                out=hid_codes[:].bitcast(E5M2),
+                scales=hid_plane[:],
+                in_=hid[:, P * u : P * (u + 1), :].rearrange("p o t -> p (o t)"),
+            )
+            for h in range(N // P):
+                bank = psum.tile([P, P], F32, name="p_bank%d%d" % (h, u))
+                nc.tensor.matmul_mx(
+                    out=bank[:],
+                    lhsT=wb_codes[:, 2 * P * h : 2 * P * (h + 1)].bitcast(E2M1),
+                    lhsT_scale=wb_plane[:, P * h : P * (h + 1)],
+                    rhs=hid_codes[:].bitcast(E5M2),
+                    rhs_scale=hid_plane[:],
+                    start=True,
+                    stop=True,
+                )
+                on_scalar(p_rows[h][:, P * u : P * (u + 1)], bank[:])
 
-        first = [tile("first%d" % h, [P, E], F32) for h in range(2)]
-        second = [tile("second%d" % h, [P, E], F32) for h in range(2)]
-        for h in range(2):
-            on_vector(first[h][:], whole[h][:].indirect(list6[:]))
-            on_scalar(second[h][:], whole[h][:].indirect(list7[:]))
-        for h, queue in ((0, nc.sync), (1, nc.scalar)):
+        first = [tile("first%d" % h, [P, E], F32) for h in range(N // P)]
+        second = [tile("second%d" % h, [P, E], F32) for h in range(N // P)]
+        for h in range(N // P):
+            on_vector(first[h][:], p_rows[h][:].indirect(first_list[:]))
+            on_scalar(second[h][:], p_rows[h][:].indirect(second_list[:]))
+        for h, queue in enumerate((nc.sync, nc.scalar)):
             larger = tile("larger%d" % h, [P, E], F32)
             nc.vector.tensor_tensor(larger[:], first[h][:], second[h][:], MAX)
             queue.dma_start(out=out[P * h : P * (h + 1), :], in_=larger[:])

from contextlib import ExitStack

import concourse.mybir as mybir

K, T, Z, J, R, C, O, N, E = 512, 1024, 1024, 256, 512, 512, 256, 256, 128
FLOPS = 2 * (4 * K * R * J + R * N * O)

F32 = mybir.dt.float32
BF16 = mybir.dt.bfloat16
I32 = mybir.dt.int32
U32 = mybir.dt.uint32
U16 = mybir.dt.uint16
U8 = mybir.dt.uint8
E4M3 = mybir.dt.float8_e4m3fn_x4
E5M2 = mybir.dt.float8_e5m2_x4
E2M1 = mybir.dt.float4_e2m1fn_x4
COPY = mybir.ActivationFunctionType.Copy
ADD = mybir.AluOpType.add
MAX = mybir.AluOpType.max

P = 128
SLOTS = 4
LINE = 16
ENTRIES = 16
BANKS = 3
PERIOD = 14
REPEATS = 5


def load_scales(first_queue, last_queue, plane, scales):
    rows = scales[0].bitcast(I32)
    words = plane.bitcast(I32)
    repeated = rows[0:PERIOD, :].unsqueeze(0).to_broadcast([REPEATS, PERIOD, rows.shape[1]])
    first_queue.dma_start(out=words[0 : PERIOD * REPEATS, :], in_=repeated)
    last_queue.dma_start(out=words[96:100, :], in_=rows[12:16, :])


def tile_list_crossed_shared_one_bestoftwo_kernel(
    tc, xt_words, xt_scales, xo_words, xo_scales, w_words, w_scales, w2_words, w2_scales,
    wb_words, wb_scales, offs, offs2, offs3, offs4, offs5, offs6, offs7, out,
):
    nc = tc.nc
    with ExitStack() as ctx:
        keep = ctx.enter_context(tc.tile_pool(name="keep", bufs=1))
        psum = ctx.enter_context(tc.psum_pool(name="psum", bufs=1))

        def tile(name, shape, dtype, tag=None):
            return keep.tile(shape, dtype, name=name, tag=tag or name, align_bytes=64)

        def load_list(name, source):
            held = keep.tile(list(source.shape), U16, name=name)
            nc.sync.dma_start(held[:], source)
            return held

        def load_words(queue, name, source, shape, dtype):
            held = tile(name, shape, dtype)
            queue.dma_start(out=held[:].bitcast(I32), in_=source.bitcast(I32))
            return held

        def flat(words):
            return words[0].rearrange("p n t -> p (n t)")

        def deal(copy, name, source, dtype, run):
            width = source.shape[1] // SLOTS
            by_slot = source.rearrange("p (c i t) -> p c t i", t=SLOTS, i=run)
            first_slot = tile(name + "_first", [P, width], dtype)
            other_slots = tile(name + "_rest", [P, (SLOTS - 1) * width], dtype)
            copy(first_slot[:].rearrange("p (c i) -> p c i", i=run), by_slot[:, :, 0, :])
            copy(other_slots[:].rearrange("p (t c i) -> p c t i", t=SLOTS - 1, i=run), by_slot[:, :, 1:SLOTS, :])
            return [first_slot[:]] + [other_slots[:, width * t : width * (t + 1)] for t in range(SLOTS - 1)]

        xt_plane = tile("xt_plane", [P, T], U8)
        xo_plane = tile("xo_plane", [P, Z], U8)
        w_planes = tile("w_planes", [P, 2 * R], U8)
        wb_plane = tile("wb_plane", [P, N], U8)
        nc.gpsimd.memset(w_planes[:].bitcast(I32), 0)
        for plane in (xt_plane, xo_plane, wb_plane):
            nc.vector.memset(plane[:].bitcast(I32), 0)

        token_list = load_list("token_list", offs)
        xt_codes = load_words(nc.scalar, "xt_codes", xt_words[0], [P, T], U16)
        note_list = load_list("note_list", offs2)
        w_codes = load_words(nc.sync, "w_codes", flat(w_words), [P, R], U32)
        xo_codes = load_words(nc.scalar, "xo_codes", flat(xo_words), [P, Z], U32)
        load_scales(nc.sync, nc.sync, xt_plane[:], xt_scales)
        load_scales(nc.sync, nc.sync, xo_plane[:], xo_scales)
        w2_codes = load_words(nc.sync, "w2_codes", flat(w2_words), [P, R], U32)
        load_scales(nc.gpsimd, nc.sync, w_planes[:, 0:R], w_scales)
        load_scales(nc.gpsimd, nc.sync, w_planes[:, R : 2 * R], w2_scales)
        places = {"a": load_list("a_places", offs3), "b": load_list("b_places", offs4)}
        read_list = load_list("read_list", offs5)
        wb_codes = load_words(nc.sync, "wb_codes", wb_words[0], [P, 2 * N], U8)
        load_scales(nc.sync, nc.sync, wb_plane[:], wb_scales)
        first_list = load_list("first_list", offs6)
        second_list = load_list("second_list", offs7)

        boards = {"a": [tile("board_a0", [P, C], F32)], "b": [tile("board_b0", [P, C], F32)]}
        nc.vector.memset(boards["a"][0][:], 0.0)
        nc.vector.memset(boards["b"][0][:], 0.0)

        words_dealt = [
            deal(nc.scalar.copy, name, codes[:], U32, LINE // 4) for name, codes in (("w", w_codes), ("w2", w2_codes))
        ]

        boards["b"].append(tile("board_b1", [P, C], F32, tag="w_codes"))
        boards["a"].append(tile("board_a1", [P, C], F32, tag="w2_codes"))
        nc.gpsimd.memset(boards["b"][1][:], 0.0)
        nc.gpsimd.memset(boards["a"][1][:], 0.0)

        xt_picked = tile("xt_picked", [P, J], U16)
        xt_picked_plane = tile("xt_picked_plane", [P, J], U8)
        nc.vector.tensor_copy(xt_picked[:], xt_codes[:].indirect(token_list[:]))
        nc.vector.tensor_copy(xt_picked_plane[:], xt_plane[:].indirect(token_list[:]))
        xo_picked = tile("xo_picked", [P, J], U32, tag="xt_plane")
        xo_picked_plane = tile("xo_picked_plane", [P, J], U8)
        nc.vector.tensor_copy(xo_picked_plane[:], xo_plane[:].indirect(note_list[:]))
        nc.vector.tensor_copy(xo_picked[:], xo_codes[:].indirect(note_list[:]))
        tokens = (xt_picked[:].bitcast(E2M1), xt_picked_plane[:])
        notes = (xo_picked[:].bitcast(E4M3), xo_picked_plane[:])

        planes_dealt = deal(nc.vector.tensor_copy, "planes", w_planes[:], U8, LINE)

        results = [("a", 0), ("b", 0), ("b", 1), ("a", 1), ("b", 2), ("a", 2), ("a", 3), ("b", 3)]
        partner = {"a": (tokens, notes), "b": (notes, tokens)}
        sums = {}

        def multiply(step):
            result, t = results[step]
            bank = psum.tile([P, J], F32, name="bank%d" % (step % BANKS))
            for matrix, fmt in ((1, E5M2), (0, E4M3)):
                codes, plane = partner[result][matrix]
                nc.tensor.matmul_mx(
                    out=bank[:],
                    lhsT=words_dealt[matrix][t].bitcast(fmt),
                    lhsT_scale=planes_dealt[t][:, matrix * P : (matrix + 1) * P],
                    rhs=codes,
                    rhs_scale=plane,
                    start=(matrix == 1),
                    stop=(matrix == 0),
                )
            sums[result, t] = bank

        def on_vector(dst, src):
            nc.vector.tensor_copy(dst, src)

        def on_scalar(dst, src):
            nc.scalar.activation(dst, src, COPY)

        staged = {}
        joined = {}
        hid = tile("hid", [P, O, SLOTS], BF16)
        half_list = P // ENTRIES

        def stage(copy, result, t):
            staged[result, t] = tile("%s%d" % (result, t), [P, J], F32)
            copy(staged[result, t][:], sums[result, t][:])
            step = results.index((result, t)) + BANKS
            if step < len(results):
                multiply(step)

        def place(copy, result, t):
            copy(boards[result][t % 2][:].indirect(places[result][:]), staged[result, t][:])

        def join(engine, t):
            joined[t] = tile("pg%d" % t, [P, C], F32)
            engine.tensor_tensor(joined[t][:], boards["a"][t % 2][:], boards["b"][t % 2][:], ADD)

        def read(t):
            nc.vector.tensor_copy(hid[:, :, t], joined[t][:].indirect(read_list[:]))

        for step in range(BANKS):
            multiply(step)

        stage(on_scalar, "a", 0)
        stage(on_scalar, "b", 0)
        place(on_vector, "a", 0)
        stage(on_scalar, "b", 1)
        place(on_scalar, "b", 0)
        stage(on_vector, "a", 1)
        stage(on_vector, "b", 2)
        join(nc.gpsimd, 0)
        place(on_vector, "a", 1)
        place(on_scalar, "b", 1)
        stage(on_vector, "a", 2)
        stage(on_vector, "a", 3)
        join(nc.gpsimd, 1)
        place(on_scalar, "b", 2)
        place(on_vector, "a", 2)
        stage(on_scalar, "b", 3)
        join(nc.gpsimd, 2)
        place(on_scalar, "a", 3)
        read(0)
        read(1)
        place(on_scalar, "b", 3)
        read(2)
        last = SLOTS - 1
        join(nc.vector, last)

        for u in range(2):
            picked = joined[last][:].indirect(read_list[:, half_list * u : half_list * (u + 1)])
            nc.vector.tensor_copy(hid[:, P * u : P * (u + 1), last], picked)

        p_rows = [tile("p%d" % h, [P, O], F32) for h in range(N // P)]
        for u in range(2):
            hid_codes = tile("hid_codes%d" % u, [P, P], U32)
            hid_plane = tile("hid_plane%d" % u, [P, P], U8)
            nc.vector.quantize_mx(
                out=hid_codes[:].bitcast(E5M2),
                scales=hid_plane[:],
                in_=hid[:, P * u : P * (u + 1), :].rearrange("p o t -> p (o t)"),
            )
            for h in range(N // P):
                bank = psum.tile([P, P], F32, name="p_bank%d%d" % (h, u))
                nc.tensor.matmul_mx(
                    out=bank[:],
                    lhsT=wb_codes[:, 2 * P * h : 2 * P * (h + 1)].bitcast(E2M1),
                    lhsT_scale=wb_plane[:, P * h : P * (h + 1)],
                    rhs=hid_codes[:].bitcast(E5M2),
                    rhs_scale=hid_plane[:],
                    start=True,
                    stop=True,
                )
                on_scalar(p_rows[h][:, P * u : P * (u + 1)], bank[:])

        first = [tile("first%d" % h, [P, E], F32) for h in range(N // P)]
        second = [tile("second%d" % h, [P, E], F32) for h in range(N // P)]
        for h in range(N // P):
            on_vector(first[h][:], p_rows[h][:].indirect(first_list[:]))
            on_scalar(second[h][:], p_rows[h][:].indirect(second_list[:]))
        for h, queue in enumerate((nc.sync, nc.scalar)):
            larger = tile("larger%d" % h, [P, E], F32)
            nc.vector.tensor_tensor(larger[:], first[h][:], second[h][:], MAX)
            queue.dma_start(out=out[P * h : P * (h + 1), :], in_=larger[:])
